import numpy as np
import ml_dtypes


def mxq(x, axis, fmt="e4m3"):
    dtype, down = {"e4m3": (ml_dtypes.float8_e4m3fn, 7), "e5m2": (ml_dtypes.float8_e5m2, 14)}[fmt]
    v = np.moveaxis(np.asarray(x, np.float32).astype(ml_dtypes.bfloat16).astype(np.float64), axis, -1)
    blocks = v.reshape(v.shape[:-1] + (-1, 32))
    amax = np.abs(blocks).max(-1, keepdims=True)
    byte = np.maximum(np.where(amax > 0, np.frexp(amax)[1] - 1 + 127, 0) - down, 1)
    scale = np.exp2(byte - 127.0)
    codes = (blocks / scale).astype(np.float32).astype(dtype).astype(np.float64)
    return np.moveaxis((codes * scale).reshape(v.shape), -1, axis)


WIDE = False


def mx_kscale(k):
    if not WIDE:
        return np.ones(k)
    levels = np.array([10, -10, 5, -5, 0])
    if k % 512:
        return np.exp2(np.random.permutation(np.resize(levels, k // 32))).repeat(32)
    a = np.empty((k // 512, 16))
    for p in range(k // 512):
        a[p, :8] = np.random.permutation(np.resize(levels, 8))
        for g in range(8):
            far = levels[np.abs(levels - a[p, g]) >= 10]
            a[p, g + 8] = far[np.random.randint(len(far))]
    return np.exp2(a.ravel()).repeat(32)


def f64(x):
    return np.asarray(x).astype(np.float64)


def striped(idx):
    return np.tile(idx.reshape(-1, 16).T, (8, 1)).astype(np.uint16)


def unstriped(offs):
    return offs[:16].T.reshape(-1).astype(np.int64)


def pack_weight(w):
    k, n = w.shape
    w = f64(np.asarray(w, np.float32).astype(ml_dtypes.bfloat16)).reshape(k // 32, 32, n)
    amax = np.abs(w).max(1)
    byte = np.clip(np.where(amax > 0, np.frexp(amax)[1] - 1 + 127 - 7, 1), 1, 254)
    scaled = (w * np.exp2(127.0 - byte)[:, None, :]).reshape(k, n).astype(np.float32)
    words = np.ascontiguousarray(scaled.reshape(k // 512, 128, 4, n).transpose(0, 1, 3, 2)).astype(ml_dtypes.float8_e4m3fn).view(np.uint8)
    return words, np.ascontiguousarray(byte.astype(np.uint8).reshape(k // 512, 16, n))


def unpack_weight(words, scales):
    g, p, n, _ = words.shape
    vals = np.ascontiguousarray(words).view(ml_dtypes.float8_e4m3fn).astype(np.float64) * np.repeat(np.exp2(scales.astype(np.float64) - 127.0), 8, axis=1)[..., None]
    return vals.transpose(0, 1, 3, 2).reshape(g * 512, n)


def relu(v):
    return np.maximum(v, 0.0)


K, T, S, V = 512, 1024, 512, 256
P = 2 ** 7


def setup_inputs():
    n = np.random.standard_normal
    s = mx_kscale(K)[:, None]
    packed_xT = pack_weight(n((K, T)) * s)
    return {
        "x_words": packed_xT[0],
        "x_scales": packed_xT[1],
        "hT": (n((K, V)) / np.sqrt(K) / s).astype(np.float32),
        "lab": (np.eye(S)[np.random.randint(0, S, V)]).astype(np.float32),
        "lcnt": (np.tile(np.random.uniform(0.0, 6.0, T), (P, 1))).astype(np.float32),
        "lown": (-np.random.uniform(0.0, 3.0, (V, 1))).astype(np.float32),
        "offs": striped(np.random.permutation(T)[:S]),
    }


def reference(x_words, x_scales, hT, lab, lcnt, lown, offs):
    hTq = mxq(f64(hT), 0, "e4m3")
    xq = unpack_weight(x_words, x_scales)[:, unstriped(offs)]
    y = 1.2 * (hTq.T @ xq)
    mit = np.minimum(0.5 * (f64(lcnt)[:1][:, unstriped(offs)]) + f64(lown), 0.05 * (f64(lcnt)[:1][:, unstriped(offs)]))
    ex = np.exp(y - y.max(axis=1, keepdims=True))
    pr = ex / ex.sum(axis=1, keepdims=True)
    pl = pr * f64(lab)
    pt = pl.sum(axis=1, keepdims=True) + 0.0005
    cmp = relu(np.log(pr / pt))
    ys = y + (-1.0 * f64(lab) + 1.0) * (mit + 0.8 * cmp)
    ex2 = np.exp(ys - ys.max(axis=1, keepdims=True))
    return 50.0 * (ex2 / ex2.sum(axis=1, keepdims=True) - f64(lab))

@@ -1,0 +1,123 @@
+import math
+from contextlib import ExitStack
+
+import concourse.mybir as mybir
+
+K, T, S, V = 512, 1024, 512, 256
+P = 128
+PACK = 4
+TILES = V // P
+FLOPS = 2 * K * V * S
+
+F32 = mybir.dt.float32
+BF16 = mybir.dt.bfloat16
+I32 = mybir.dt.int32
+U32 = mybir.dt.uint32
+U16 = mybir.dt.uint16
+U8 = mybir.dt.uint8
+FP8X4 = mybir.dt.float8_e4m3fn_x4
+ALU = mybir.AluOpType
+ACT = mybir.ActivationFunctionType
+
+SCORE = 1.2
+EPS = 0.0005
+POWER = 0.8
+GRAD = 50.0
+
+
+def tile_picked_yseesw_grad_p_kernel(tc, x_words, x_scales, hT, lab, lcnt, lown, offs, out):
+    nc = tc.nc
+    with ExitStack() as ctx:
+        keep = ctx.enter_context(tc.tile_pool(name="keep", bufs=1))
+        psum = ctx.enter_context(tc.psum_pool(name="psum", bufs=1))
+
+        def wide(name):
+            return [keep.tile([P, S], F32, name="%s%d" % (name, i)) for i in range(TILES)]
+
+        def column(name):
+            return [keep.tile([P, 1], F32, name="%s%d" % (name, i)) for i in range(TILES)]
+
+        offsets = keep.tile([P, S // 16], U16, name="offsets")
+        scale_win = keep.tile([P, T], U8, name="scale_win", align_bytes=64)
+        word_win = keep.tile([P, T], U32, name="word_win", align_bytes=64)
+        count_win = keep.tile([P, T], F32, name="count_win", align_bytes=64)
+        h_raw = keep.tile([P, PACK, V], F32, name="h_raw")
+        own = keep.tile([P, TILES], F32, name="own")
+        label = wide("label")
+
+        ones = keep.tile([P, 1], F32, name="ones")
+        warm = keep.tile([P, 1], F32, name="warm")
+        power = keep.tile([P, 1], F32, name="power")
+        nc.gpsimd.memset(scale_win[:].bitcast(I32), 0)
+        nc.gpsimd.memset(ones[:], 1.0)
+        nc.scalar.activation(warm[:], ones[:], ACT.Exp)
+        nc.gpsimd.tensor_scalar(power[:], ones[:], POWER, 0.0, ALU.mult, ALU.add)
+
+        nc.sync.dma_start(offsets[:], offs)
+        for q in range(4):
+            nc.sync.dma_start(scale_win[32 * q : 32 * q + 4, :].bitcast(I32), x_scales[0, 4 * q : 4 * q + 4, :].bitcast(I32))
+        with nc.allow_non_contiguous_dma(reason="one value a row"):
+            nc.sync.dma_start(own[:], lown.rearrange("(i p) o -> p (i o)", p=P))
+        nc.sync.dma_start(count_win[:], lcnt)
+        nc.sync.dma_start(word_win[:].bitcast(I32), x_words[0].rearrange("p n t -> p (n t)").bitcast(I32))
+        nc.sync.dma_start(h_raw[:], hT.rearrange("(p j) v -> p j v", j=PACK))
+        for i in range(TILES):
+            nc.sync.dma_start(label[i][:], lab[i * P : (i + 1) * P, :])
+
+        x_scale = keep.tile([P, S], U8, name="x_scale", align_bytes=64)
+        x_code = keep.tile([P, S], U32, name="x_code", align_bytes=64)
+        count = keep.tile([P, S], F32, name="count")
+        nc.vector.tensor_copy(x_scale[:], scale_win[:].indirect(offsets[:]))
+        nc.vector.tensor_copy(count[:], count_win[:].indirect(offsets[:]))
+        nc.vector.tensor_copy(x_code[:], word_win[:].indirect(offsets[:]))
+
+        tenth = keep.tile([P, S], F32, name="tenth")
+        own2 = keep.tile([P, TILES], F32, name="own2")
+        nc.scalar.activation(tenth[:], count[:], ACT.Copy, scale=0.1)
+        nc.gpsimd.tensor_scalar(own2[:], own[:], 2.0, 0.0, ALU.mult, ALU.add)
+
+        bank = []
+        for i in range(TILES):
+            h_bf = keep.tile([P, P, PACK], BF16, name="h_bf%d" % i, align_bytes=64)
+            h_code = keep.tile([P, P], U32, name="h_code%d" % i, align_bytes=64)
+            h_scale = keep.tile([P, P], U8, name="h_scale%d" % i, align_bytes=64)
+            nc.scalar.copy(h_bf[:], h_raw[:, :, i * P : (i + 1) * P].rearrange("p j m -> p m j"))
+            nc.vector.quantize_mx(out=h_code[:].bitcast(FP8X4), scales=h_scale[:], in_=h_bf[:].rearrange("p m j -> p (m j)"))
+            acc = psum.tile([P, S], F32, name="acc%d" % i)
+            nc.tensor.matmul_mx(out=acc[:], lhsT=h_code[:].bitcast(FP8X4), lhsT_scale=h_scale[:],
+                                rhs=x_code[:].bitcast(FP8X4), rhs_scale=x_scale[:], start=True, stop=True)
+            bank.append(acc)
+
+        mit2, shift2, others = wide("mit2"), wide("shift2"), wide("others")
+        neg_y, lifted, moved = wide("neg_y"), wide("lifted"), wide("moved")
+        spent, sharp, soft, weight, result = wide("spent"), wide("sharp"), wide("soft"), wide("weight"), wide("result")
+        neg_max, sharp_bias, denom, floor = column("neg_max"), column("sharp_bias"), column("denom"), column("floor")
+        total, inv, gain = column("total"), column("inv"), column("gain")
+
+        for i in range(TILES):
+            nc.vector.scalar_tensor_tensor(mit2[i][:], count[:], own2[:, i : i + 1], tenth[:], ALU.add, ALU.min)
+        for i in range(TILES):
+            nc.scalar.activation(others[i][:], label[i][:], ACT.Copy, scale=-1.0, bias=1.0)
+            nc.gpsimd.tensor_tensor(shift2[i][:], mit2[i][:], others[i][:], ALU.mult)
+        for i in range(TILES):
+            nc.vector.tensor_scalar(neg_y[i][:], bank[i][:], -SCORE, None, ALU.mult, ALU.min, accum_out=neg_max[i][:])
+            nc.scalar.activation(sharp_bias[i][:], neg_max[i][:], ACT.Identity, scale=POWER, bias=-POWER * math.log(EPS))
+            nc.scalar.activation(sharp[i][:], neg_y[i][:], ACT.Exp, scale=-POWER, bias=sharp_bias[i][:])
+            nc.vector.scalar_tensor_tensor(lifted[i][:], label[i][:], math.log((1.0 + EPS) / EPS) / SCORE, bank[i][:], ALU.mult, ALU.add)
+            nc.scalar.activation(spent[i][:], lifted[i][:], ACT.Exp, scale=SCORE, bias=neg_max[i][:], accum_out=denom[i][:])
+            nc.gpsimd.tensor_tensor(floor[i][:], denom[i][:], power[:], ALU.pow)
+            nc.vector.scalar_tensor_tensor(moved[i][:], shift2[i][:], 0.5 / SCORE, bank[i][:], ALU.mult, ALU.add)
+            nc.scalar.activation(soft[i][:], moved[i][:], ACT.Exp, scale=SCORE, bias=neg_max[i][:])
+        label50 = [moved[TILES - 1], lifted[TILES - 1]]
+        for i in range(TILES):
+            nc.scalar.activation(label50[i][:], label[i][:], ACT.Copy, scale=GRAD)
+        for i in range(TILES):
+            nc.vector.scalar_tensor_tensor(weight[i][:], sharp[i][:], floor[i][:], soft[i][:], ALU.max, ALU.mult, accum_out=total[i][:])
+        for i in range(TILES):
+            nc.vector.reciprocal(inv[i][:], total[i][:])
+            nc.vector.tensor_scalar(gain[i][:], inv[i][:], GRAD, None, ALU.mult)
+        for i in range(TILES):
+            for half in range(2):
+                cols = slice(half * S // 2, (half + 1) * S // 2)
+                nc.vector.scalar_tensor_tensor(result[i][:, cols], weight[i][:, cols], gain[i][:], label50[i][:, cols], ALU.mult, ALU.subtract)
+                nc.sync.dma_start(out[i * P : (i + 1) * P, cols], result[i][:, cols])

@@ -23,6 +23,7 @@ SCORE = 1.2
 EPS = 0.0005
 POWER = 0.8
 GRAD = 50.0
+HALVES = (slice(0, S // 2), slice(S // 2, S))
 
 
 def tile_picked_yseesw_grad_p_kernel(tc, x_words, x_scales, hT, lab, lcnt, lown, offs, out):
@@ -78,7 +79,7 @@ def tile_picked_yseesw_grad_p_kernel(tc, x_words, x_scales, hT, lab, lcnt, lown,
 
         bank = []
         for i in range(TILES):
-            h_bf = keep.tile([P, P, PACK], BF16, name="h_bf%d" % i, align_bytes=64)
+            h_bf = keep.tile([P, P, PACK], BF16, name="h_bf%d" % i, tag="turn%d" % i, align_bytes=64)
             h_code = keep.tile([P, P], U32, name="h_code%d" % i, align_bytes=64)
             h_scale = keep.tile([P, P], U8, name="h_scale%d" % i, align_bytes=64)
             nc.scalar.copy(h_bf[:], h_raw[:, :, i * P : (i + 1) * P].rearrange("p j m -> p m j"))
@@ -88,36 +89,55 @@ def tile_picked_yseesw_grad_p_kernel(tc, x_words, x_scales, hT, lab, lcnt, lown,
                                 rhs=x_code[:].bitcast(FP8X4), rhs_scale=x_scale[:], start=True, stop=True)
             bank.append(acc)
 
-        mit2, shift2, others = wide("mit2"), wide("shift2"), wide("others")
-        neg_y, lifted, moved = wide("neg_y"), wide("lifted"), wide("moved")
+        others = wide("others")
+        mit2 = [keep.tile([P, S], F32, name="mit2_0", tag="turn0", align_bytes=64), keep.tile([P, S], F32, name="mit2_1")]
+        shift2 = wide("shift2")
+        neg_y, lifted = wide("neg_y"), wide("lifted")
+        moved = wide("moved")
         spent, sharp, soft, weight, result = wide("spent"), wide("sharp"), wide("soft"), wide("weight"), wide("result")
-        neg_max, sharp_bias, denom, floor = column("neg_max"), column("sharp_bias"), column("denom"), column("floor")
-        total, inv, gain = column("total"), column("inv"), column("gain")
+        neg_max, denom, floor = column("neg_max"), column("denom"), column("floor")
+        total, gain = column("total"), column("gain")
+        parts = [keep.tile([P, 2], F32, name="parts%d" % i) for i in range(TILES)]
 
-        for i in range(TILES):
+        for i in reversed(range(TILES)):
             nc.vector.scalar_tensor_tensor(mit2[i][:], count[:], own2[:, i : i + 1], tenth[:], ALU.add, ALU.min)
         for i in range(TILES):
             nc.scalar.activation(others[i][:], label[i][:], ACT.Copy, scale=-1.0, bias=1.0)
             nc.gpsimd.tensor_tensor(shift2[i][:], mit2[i][:], others[i][:], ALU.mult)
+        label50 = [keep.tile([P, S], F32, name="label50_0"), moved[1]]
+        nc.scalar.activation(label50[0][:], label[0][:], ACT.Copy, scale=GRAD)
+        sharp_bias = [label[0][:, 0:1], keep.tile([P, 1], F32, name="sharp_bias1")]
+
+        def sharpen(i):
+            nc.scalar.activation(sharp[i][:], neg_y[i][:], ACT.Exp, scale=-POWER, bias=sharp_bias[i][:])
+
+        def soften(i):
+            nc.vector.scalar_tensor_tensor(moved[i][:], shift2[i][:], 0.5 / SCORE, bank[i][:], ALU.mult, ALU.add)
+            for cols in HALVES:
+                nc.scalar.activation(soft[i][:, cols], moved[i][:, cols], ACT.Exp, scale=SCORE, bias=neg_max[i][:])
+
+        def weigh(i):
+            for half, cols in enumerate(HALVES):
+                nc.vector.scalar_tensor_tensor(weight[i][:, cols], sharp[i][:, cols], floor[i][:], soft[i][:, cols], ALU.max, ALU.mult,
+                                               accum_out=parts[i][:, half : half + 1])
+            nc.vector.tensor_scalar(total[i][:], parts[i][:, 0:1], parts[i][:, 1:2], 1.0 / GRAD, ALU.add, ALU.mult)
+            nc.vector.reciprocal(gain[i][:], total[i][:])
+
         for i in range(TILES):
             nc.vector.tensor_scalar(neg_y[i][:], bank[i][:], -SCORE, None, ALU.mult, ALU.min, accum_out=neg_max[i][:])
-            nc.scalar.activation(sharp_bias[i][:], neg_max[i][:], ACT.Identity, scale=POWER, bias=-POWER * math.log(EPS))
-            nc.scalar.activation(sharp[i][:], neg_y[i][:], ACT.Exp, scale=-POWER, bias=sharp_bias[i][:])
-            nc.vector.scalar_tensor_tensor(lifted[i][:], label[i][:], math.log((1.0 + EPS) / EPS) / SCORE, bank[i][:], ALU.mult, ALU.add)
+            nc.scalar.activation(sharp_bias[i][:], neg_max[i][:], ACT.Identity, scale=POWER, bias=-POWER * math.log(1.0 + EPS))
+            if i == 0:
+                sharpen(0)
+            nc.vector.scalar_tensor_tensor(lifted[i][:], others[i][:], -math.log((1.0 + EPS) / EPS) / SCORE, bank[i][:], ALU.mult, ALU.add)
             nc.scalar.activation(spent[i][:], lifted[i][:], ACT.Exp, scale=SCORE, bias=neg_max[i][:], accum_out=denom[i][:])
             nc.gpsimd.tensor_tensor(floor[i][:], denom[i][:], power[:], ALU.pow)
-            nc.vector.scalar_tensor_tensor(moved[i][:], shift2[i][:], 0.5 / SCORE, bank[i][:], ALU.mult, ALU.add)
-            nc.scalar.activation(soft[i][:], moved[i][:], ACT.Exp, scale=SCORE, bias=neg_max[i][:])
-        label50 = [moved[TILES - 1], lifted[TILES - 1]]
+        soften(0)
+        sharpen(1)
+        soften(1)
+        nc.scalar.activation(label50[1][:], label[1][:], ACT.Copy, scale=GRAD)
         for i in range(TILES):
-            nc.scalar.activation(label50[i][:], label[i][:], ACT.Copy, scale=GRAD)
+            weigh(i)
         for i in range(TILES):
-            nc.vector.scalar_tensor_tensor(weight[i][:], sharp[i][:], floor[i][:], soft[i][:], ALU.max, ALU.mult, accum_out=total[i][:])
-        for i in range(TILES):
-            nc.vector.reciprocal(inv[i][:], total[i][:])
-            nc.vector.tensor_scalar(gain[i][:], inv[i][:], GRAD, None, ALU.mult)
-        for i in range(TILES):
-            for half in range(2):
-                cols = slice(half * S // 2, (half + 1) * S // 2)
+            for cols in HALVES:
                 nc.vector.scalar_tensor_tensor(result[i][:, cols], weight[i][:, cols], gain[i][:], label50[i][:, cols], ALU.mult, ALU.subtract)
                 nc.sync.dma_start(out[i * P : (i + 1) * P, cols], result[i][:, cols])

@@ -55,22 +55,22 @@ def tile_picked_yseesw_grad_p_kernel(tc, x_words, x_scales, hT, lab, lcnt, lown,
         nc.gpsimd.tensor_scalar(power[:], ones[:], POWER, 0.0, ALU.mult, ALU.add)
 
         nc.sync.dma_start(offsets[:], offs)
-        for q in range(4):
-            nc.sync.dma_start(scale_win[32 * q : 32 * q + 4, :].bitcast(I32), x_scales[0, 4 * q : 4 * q + 4, :].bitcast(I32))
-        with nc.allow_non_contiguous_dma(reason="one value a row"):
-            nc.sync.dma_start(own[:], lown.rearrange("(i p) o -> p (i o)", p=P))
         nc.sync.dma_start(count_win[:], lcnt)
         nc.sync.dma_start(word_win[:].bitcast(I32), x_words[0].rearrange("p n t -> p (n t)").bitcast(I32))
+        for q in range(4):
+            nc.sync.dma_start(scale_win[32 * q : 32 * q + 4, :].bitcast(I32), x_scales[0, 4 * q : 4 * q + 4, :].bitcast(I32))
         nc.sync.dma_start(h_raw[:], hT.rearrange("(p j) v -> p j v", j=PACK))
+        with nc.allow_non_contiguous_dma(reason="one value a row"):
+            nc.sync.dma_start(own[:], lown.rearrange("(i p) o -> p (i o)", p=P))
         for i in range(TILES):
             nc.sync.dma_start(label[i][:], lab[i * P : (i + 1) * P, :])
 
         x_scale = keep.tile([P, S], U8, name="x_scale", align_bytes=64)
         x_code = keep.tile([P, S], U32, name="x_code", align_bytes=64)
         count = keep.tile([P, S], F32, name="count")
-        nc.vector.tensor_copy(x_scale[:], scale_win[:].indirect(offsets[:]))
         nc.vector.tensor_copy(count[:], count_win[:].indirect(offsets[:]))
         nc.vector.tensor_copy(x_code[:], word_win[:].indirect(offsets[:]))
+        nc.vector.tensor_copy(x_scale[:], scale_win[:].indirect(offsets[:]))
 
         tenth = keep.tile([P, S], F32, name="tenth")
         own2 = keep.tile([P, TILES], F32, name="own2")

import math
from contextlib import ExitStack

import concourse.mybir as mybir

K, T, S, V = 512, 1024, 512, 256
P = 128
PACK = 4
TILES = V // P
FLOPS = 2 * K * V * S

F32 = mybir.dt.float32
BF16 = mybir.dt.bfloat16
I32 = mybir.dt.int32
U32 = mybir.dt.uint32
U16 = mybir.dt.uint16
U8 = mybir.dt.uint8
FP8X4 = mybir.dt.float8_e4m3fn_x4
ALU = mybir.AluOpType
ACT = mybir.ActivationFunctionType

SCORE = 1.2
EPS = 0.0005
POWER = 0.8
GRAD = 50.0
HALVES = (slice(0, S // 2), slice(S // 2, S))


def tile_picked_yseesw_grad_p_kernel(tc, x_words, x_scales, hT, lab, lcnt, lown, offs, out):
    nc = tc.nc
    with ExitStack() as ctx:
        keep = ctx.enter_context(tc.tile_pool(name="keep", bufs=1))
        psum = ctx.enter_context(tc.psum_pool(name="psum", bufs=1))

        def wide(name):
            return [keep.tile([P, S], F32, name="%s%d" % (name, i)) for i in range(TILES)]

        def column(name):
            return [keep.tile([P, 1], F32, name="%s%d" % (name, i)) for i in range(TILES)]

        offsets = keep.tile([P, S // 16], U16, name="offsets")
        scale_win = keep.tile([P, T], U8, name="scale_win", align_bytes=64)
        word_win = keep.tile([P, T], U32, name="word_win", align_bytes=64)
        count_win = keep.tile([P, T], F32, name="count_win", align_bytes=64)
        h_raw = keep.tile([P, PACK, V], F32, name="h_raw")
        own = keep.tile([P, TILES], F32, name="own")
        label = wide("label")

        ones = keep.tile([P, 1], F32, name="ones")
        warm = keep.tile([P, 1], F32, name="warm")
        power = keep.tile([P, 1], F32, name="power")
        nc.gpsimd.memset(scale_win[:].bitcast(I32), 0)
        nc.gpsimd.memset(ones[:], 1.0)
        nc.scalar.activation(warm[:], ones[:], ACT.Exp)
        nc.gpsimd.tensor_scalar(power[:], ones[:], POWER, 0.0, ALU.mult, ALU.add)

        nc.sync.dma_start(offsets[:], offs)
        nc.sync.dma_start(count_win[:], lcnt)
        nc.sync.dma_start(word_win[:].bitcast(I32), x_words[0].rearrange("p n t -> p (n t)").bitcast(I32))
        for q in range(4):
            nc.sync.dma_start(scale_win[32 * q : 32 * q + 4, :].bitcast(I32), x_scales[0, 4 * q : 4 * q + 4, :].bitcast(I32))
        nc.sync.dma_start(h_raw[:], hT.rearrange("(p j) v -> p j v", j=PACK))
        with nc.allow_non_contiguous_dma(reason="one value a row"):
            nc.sync.dma_start(own[:], lown.rearrange("(i p) o -> p (i o)", p=P))
        for i in range(TILES):
            nc.sync.dma_start(label[i][:], lab[i * P : (i + 1) * P, :])

        x_scale = keep.tile([P, S], U8, name="x_scale", align_bytes=64)
        x_code = keep.tile([P, S], U32, name="x_code", align_bytes=64)
        count = keep.tile([P, S], F32, name="count")
        nc.vector.tensor_copy(count[:], count_win[:].indirect(offsets[:]))
        nc.vector.tensor_copy(x_code[:], word_win[:].indirect(offsets[:]))
        nc.vector.tensor_copy(x_scale[:], scale_win[:].indirect(offsets[:]))

        tenth = keep.tile([P, S], F32, name="tenth")
        own2 = keep.tile([P, TILES], F32, name="own2")
        nc.scalar.activation(tenth[:], count[:], ACT.Copy, scale=0.1)
        nc.gpsimd.tensor_scalar(own2[:], own[:], 2.0, 0.0, ALU.mult, ALU.add)

        bank = []
        for i in range(TILES):
            h_bf = keep.tile([P, P, PACK], BF16, name="h_bf%d" % i, tag="turn%d" % i, align_bytes=64)
            h_code = keep.tile([P, P], U32, name="h_code%d" % i, align_bytes=64)
            h_scale = keep.tile([P, P], U8, name="h_scale%d" % i, align_bytes=64)
            nc.scalar.copy(h_bf[:], h_raw[:, :, i * P : (i + 1) * P].rearrange("p j m -> p m j"))
            nc.vector.quantize_mx(out=h_code[:].bitcast(FP8X4), scales=h_scale[:], in_=h_bf[:].rearrange("p m j -> p (m j)"))
            acc = psum.tile([P, S], F32, name="acc%d" % i)
            nc.tensor.matmul_mx(out=acc[:], lhsT=h_code[:].bitcast(FP8X4), lhsT_scale=h_scale[:],
                                rhs=x_code[:].bitcast(FP8X4), rhs_scale=x_scale[:], start=True, stop=True)
            bank.append(acc)

        others = wide("others")
        mit2 = [keep.tile([P, S], F32, name="mit2_0", tag="turn0", align_bytes=64), keep.tile([P, S], F32, name="mit2_1")]
        shift2 = wide("shift2")
        neg_y, lifted = wide("neg_y"), wide("lifted")
        moved = wide("moved")
        spent, sharp, soft, weight, result = wide("spent"), wide("sharp"), wide("soft"), wide("weight"), wide("result")
        neg_max, denom, floor = column("neg_max"), column("denom"), column("floor")
        total, gain = column("total"), column("gain")
        parts = [keep.tile([P, 2], F32, name="parts%d" % i) for i in range(TILES)]

        for i in reversed(range(TILES)):
            nc.vector.scalar_tensor_tensor(mit2[i][:], count[:], own2[:, i : i + 1], tenth[:], ALU.add, ALU.min)
        for i in range(TILES):
            nc.scalar.activation(others[i][:], label[i][:], ACT.Copy, scale=-1.0, bias=1.0)
            nc.gpsimd.tensor_tensor(shift2[i][:], mit2[i][:], others[i][:], ALU.mult)
        label50 = [keep.tile([P, S], F32, name="label50_0"), moved[1]]
        nc.scalar.activation(label50[0][:], label[0][:], ACT.Copy, scale=GRAD)
        sharp_bias = [label[0][:, 0:1], keep.tile([P, 1], F32, name="sharp_bias1")]

        def sharpen(i):
            nc.scalar.activation(sharp[i][:], neg_y[i][:], ACT.Exp, scale=-POWER, bias=sharp_bias[i][:])

        def soften(i):
            nc.vector.scalar_tensor_tensor(moved[i][:], shift2[i][:], 0.5 / SCORE, bank[i][:], ALU.mult, ALU.add)
            for cols in HALVES:
                nc.scalar.activation(soft[i][:, cols], moved[i][:, cols], ACT.Exp, scale=SCORE, bias=neg_max[i][:])

        def weigh(i):
            for half, cols in enumerate(HALVES):
                nc.vector.scalar_tensor_tensor(weight[i][:, cols], sharp[i][:, cols], floor[i][:], soft[i][:, cols], ALU.max, ALU.mult,
                                               accum_out=parts[i][:, half : half + 1])
            nc.vector.tensor_scalar(total[i][:], parts[i][:, 0:1], parts[i][:, 1:2], 1.0 / GRAD, ALU.add, ALU.mult)
            nc.vector.reciprocal(gain[i][:], total[i][:])

        for i in range(TILES):
            nc.vector.tensor_scalar(neg_y[i][:], bank[i][:], -SCORE, None, ALU.mult, ALU.min, accum_out=neg_max[i][:])
            nc.scalar.activation(sharp_bias[i][:], neg_max[i][:], ACT.Identity, scale=POWER, bias=-POWER * math.log(1.0 + EPS))
            if i == 0:
                sharpen(0)
            nc.vector.scalar_tensor_tensor(lifted[i][:], others[i][:], -math.log((1.0 + EPS) / EPS) / SCORE, bank[i][:], ALU.mult, ALU.add)
            nc.scalar.activation(spent[i][:], lifted[i][:], ACT.Exp, scale=SCORE, bias=neg_max[i][:], accum_out=denom[i][:])
            nc.gpsimd.tensor_tensor(floor[i][:], denom[i][:], power[:], ALU.pow)
        soften(0)
        sharpen(1)
        soften(1)
        nc.scalar.activation(label50[1][:], label[1][:], ACT.Copy, scale=GRAD)
        for i in range(TILES):
            weigh(i)
        for i in range(TILES):
            for cols in HALVES:
                nc.vector.scalar_tensor_tensor(result[i][:, cols], weight[i][:, cols], gain[i][:], label50[i][:, cols], ALU.mult, ALU.subtract)
                nc.sync.dma_start(out[i * P : (i + 1) * P, cols], result[i][:, cols])
